import numpy as np
import ml_dtypes


def mxq(x, axis, fmt="e4m3"):
    dtype, down = {"e4m3": (ml_dtypes.float8_e4m3fn, 7), "e5m2": (ml_dtypes.float8_e5m2, 14)}[fmt]
    v = np.moveaxis(np.asarray(x, np.float32).astype(ml_dtypes.bfloat16).astype(np.float64), axis, -1)
    blocks = v.reshape(v.shape[:-1] + (-1, 32))
    amax = np.abs(blocks).max(-1, keepdims=True)
    byte = np.maximum(np.where(amax > 0, np.frexp(amax)[1] - 1 + 127, 0) - down, 1)
    scale = np.exp2(byte - 127.0)
    codes = (blocks / scale).astype(np.float32).astype(dtype).astype(np.float64)
    return np.moveaxis((codes * scale).reshape(v.shape), -1, axis)


WIDE = False


def mx_kscale(k):
    if not WIDE:
        return np.ones(k)
    levels = np.array([10, -10, 5, -5, 0])
    if k % 512:
        return np.exp2(np.random.permutation(np.resize(levels, k // 32))).repeat(32)
    a = np.empty((k // 512, 16))
    for p in range(k // 512):
        a[p, :8] = np.random.permutation(np.resize(levels, 8))
        for g in range(8):
            far = levels[np.abs(levels - a[p, g]) >= 10]
            a[p, g + 8] = far[np.random.randint(len(far))]
    return np.exp2(a.ravel()).repeat(32)


BF16 = ml_dtypes.bfloat16


def bf(x):
    return np.asarray(x, np.float32).astype(BF16)


def f64(x):
    return np.asarray(x).astype(np.float64)


E2M1 = np.array([0.0, 0.5, 1.0, 1.5, 2.0, 3.0, 4.0, 6.0, -0.0, -0.5, -1.0, -1.5, -2.0, -3.0, -4.0, -6.0])


def pack_weight(w, fmt):
    k, n = w.shape
    w = f64(bf(w)).reshape(k // 32, 32, n)
    amax = np.abs(w).max(1)
    if fmt == "e4m3":
        byte = np.frexp(amax)[1] - 1 + 127 - 7
    else:
        mant, ex = np.frexp(amax / 6.0)
        byte = np.where(mant > 0.5, ex, ex - 1) + 127
    byte = np.clip(np.where(amax > 0, byte, 1), 1, 254)
    scaled = (w * np.exp2(127.0 - byte)[:, None, :]).reshape(k, n).astype(np.float32)
    by_word = np.ascontiguousarray(scaled.reshape(k // 512, 128, 4, n).transpose(0, 1, 3, 2))
    if fmt == "e4m3":
        words = by_word.astype(ml_dtypes.float8_e4m3fn).view(np.uint8)
    else:
        c = by_word.astype(ml_dtypes.float4_e2m1fn).view(np.uint8) & 0xF
        words = c[..., 0::2] | (c[..., 1::2] << 4)
    return np.ascontiguousarray(words), np.ascontiguousarray(byte.astype(np.uint8).reshape(k // 512, 16, n))


def unpack_weight(words, scales, fmt):
    g, p, n, _ = words.shape
    if fmt == "e4m3":
        vals = np.ascontiguousarray(words).view(ml_dtypes.float8_e4m3fn).astype(np.float64)
    else:
        nib = np.empty((g, p, n, 4), np.uint8)
        nib[..., 0::2] = words & 0xF
        nib[..., 1::2] = words >> 4
        vals = E2M1[nib]
    vals = vals * np.repeat(np.exp2(scales.astype(np.float64) - 127.0), 8, axis=1)[..., None]
    return vals.transpose(0, 1, 3, 2).reshape(g * 512, n)
def pack4(w):
    words, scales = pack_weight(w, "e2m1")
    return words.reshape(words.shape[0], 128, -1), scales


def unpack4(words, scales):
    return unpack_weight(words.reshape(words.shape[0], 128, -1, 2), scales, "e2m1")


def planes(Y):
    n, m = Y.shape
    b = f64(bf(Y)).reshape(n // 32, 32, m)
    amax = np.abs(b).max(1)
    byte = np.clip(np.where(amax > 0, np.frexp(amax)[1] - 1 + 127 - 7, 1), 1, 254)
    codes = (b * np.exp2(127.0 - byte)[:, None, :]).reshape(n, m).astype(np.float32).astype(ml_dtypes.float8_e4m3fn).view(np.uint8)
    words = codes.reshape(n // 512, 128, 4, m).transpose(0, 1, 3, 2)
    return np.ascontiguousarray(words), np.ascontiguousarray(byte.astype(np.uint8).reshape(n // 512, 16, m))


TOK, FIN, DIN, DOUT, FNX = 1536, 512, 1024, 1024, 1024

def sigmoid(z):
    return 1.0 / (1.0 + np.exp(-z))

def setup_inputs():
    s = mx_kscale(FIN)
    u = mx_kscale(FNX)
    v = mx_kscale(TOK)
    x = bf(np.random.randn(TOK, FIN) * s[None, :])
    a = bf(np.random.randn(FIN, DIN) / np.sqrt(FIN) / s[:, None])
    token_gate = bf(np.exp(0.3 * np.random.randn(TOK, 1)) * v[:, None])
    loss_weight = bf(np.exp(0.3 * np.random.randn(TOK, 1)) / v[:, None])
    e_words, e_scales = pack_weight(0.1 * np.random.randn(FNX, TOK) * u[:, None], "e4m3")
    b_words, b_scales = pack4(np.random.randn(FNX, DOUT) / np.sqrt(FNX) / u[:, None])
    spread = np.exp(np.random.uniform(-1.2, 1.2, (DIN, 1)))
    w = bf(0.5 * spread * np.random.randn(DIN, DOUT))
    score = bf(np.random.randn(DIN, DOUT))
    return dict(x=x, a=a, token_gate=token_gate, loss_weight=loss_weight, e_words=e_words, e_scales=e_scales,
                b_words=b_words, b_scales=b_scales, w=w, score=score)

def reference(x, a, token_gate, loss_weight, e_words, e_scales, b_words, b_scales, w, score):
    z = mxq(f64(x), 1) @ mxq(f64(a), 0)
    h = z * sigmoid(z) * f64(token_gate)
    et = unpack_weight(e_words, e_scales, "e4m3")
    bt = unpack4(b_words, b_scales)
    d = (et.T @ bt) * f64(loss_weight)
    grad = mxq(h, 0).T @ mxq(d, 0)
    wf = f64(w)
    y = wf * sigmoid(f64(score) - grad * wf)
    Y = y
    words, scales = planes(Y)
    return y, words, scales

from contextlib import ExitStack

import concourse.mybir as mybir
from concourse.masks import make_identity

TOK, FIN, DIN, DOUT, FNX = 1536, 512, 1024, 1024, 1024
FLOPS = 2 * TOK * FIN * DIN + 2 * TOK * FNX * DOUT + 2 * DIN * TOK * DOUT

F32 = mybir.dt.float32
BF16 = mybir.dt.bfloat16
I32 = mybir.dt.int32
U32 = mybir.dt.uint32
U8 = mybir.dt.uint8
FP8X4 = mybir.dt.float8_e4m3fn_x4
FP4X4 = mybir.dt.float4_e2m1fn_x4
ALU = mybir.AluOpType
ACT = mybir.ActivationFunctionType

P = 128
KP = 512
NG = TOK // KP

MIX_BUFS = 6
WIDE_BUFS = 10
FIXED = ("setup", "ld_fac")
ON_S = [(2, 0), (0, 1), (1, 1), (2, 1)]
POOL_H = []
POOL_Y = []


def order():
    return [('ld_fac',),
        ('ld_x', 2),
        ('setup',),
        ('ld_x', 0),
        ('ld_x', 1),
        ('warm_up', ACT.Silu),
        ('x_turn', 2, 0),
        ('x_turn', 2, 1),
        ('ld_a', 0),
        ('ld_a', 1),
        ('x_turn', 0, 0),
        ('x_turn', 1, 0),
        ('x_turn', 1, 1),
        ('x_quant', 2),
        ('ld_e', 0),
        ('a_mix', 0, True),
        ('x_turn', 0, 1),
        ('ld_e', 2),
        ('ld_es',),
        ('a_mix', 1, False),
        ('x_quant', 1),
        ('a_quant', 0),
        ('ld_bs',),
        ('z_silu', 2, 0, 0),
        ('x_quant', 0),
        ('z_silu', 2, 0, 1),
        ('e_perm', 0),
        ('z_silu', 1, 0, 0),
        ('fac_a',),
        ('e_perm', 2),
        ('a_quant', 1),
        ('fac_b',),
        ('z_silu', 0, 0, 0),
        ('z_silu', 0, 0, 1),
        ('ld_b', 0),
        ('ld_e', 1),
        ('es_perm',),
        ('h_gate', 2, 0, 0, 0, 4, False),
        ('ld_b', 1),
        ('z_silu', 0, 0, 2),
        ('z_silu', 2, 0, 2),
        ('h_gate', 0, 0, 0, 0, 4, False),
        ('d_vec', 0, 0, 0),
        ('z_silu', 1, 0, 1),
        ('z_silu', 1, 0, 2),
        ('e_perm', 1),
        ('z_silu', 2, 0, 3),
        ('h_gate', 1, 0, 0, 0, 4, False),
        ('d_vec', 0, 0, 3),
        ('z_silu', 1, 0, 3),
        ('h_gate', 1, 0, 1, 0, 4, False),
        ('d_act', 2, 0, 0),
        ('h_gate', 2, 0, 1, 0, 4, False),
        ('z_silu', 0, 1, 2),
        ('d_act', 2, 0, 2),
        ('d_vec', 0, 0, 2),
        ('z_silu', 0, 0, 3),
        ('z_silu', 2, 1, 2),
        ('z_silu', 1, 1, 0),
        ('z_silu', 2, 1, 0),
        ('d_vec', 1, 0, 0),
        ('d_act', 2, 0, 1),
        ('ld_ws', 1),
        ('z_silu', 0, 1, 0),
        ('z_silu', 1, 1, 1),
        ('h_quant', 1, 0),
        ('h_gate', 0, 0, 1, 0, 4, False),
        ('d_vec', 1, 0, 2),
        ('d_act', 1, 1, 0),
        ('d_act', 2, 0, 3),
        ('h_quant', 2, 0),
        ('h_gate', 1, 1, 0, 0, 4, False),
        ('z_silu', 2, 1, 1),
        ('d_mix', 2, 0),
        ('ld_ws', 0),
        ('z_silu', 0, 1, 1),
        ('d_vec', 0, 0, 1),
        ('z_silu', 2, 1, 3),
        ('h_quant', 0, 0),
        ('d_vec', 1, 0, 1),
        ('d_vec', 1, 0, 3),
        ('d_quant', 0, 0),
        ('h_gate', 2, 1, 0, 0, 4, False),
        ('d_act', 0, 1, 0),
        ('h_gate', 0, 1, 0, 0, 4, False),
        ('z_silu', 1, 1, 2),
        ('d_act', 0, 1, 1),
        ('d_quant', 2, 0),
        ('z_silu', 1, 1, 3),
        ('z_silu', 0, 1, 3),
        ('d_quant', 1, 0),
        ('d_act', 1, 1, 2),
        ('d_act', 1, 1, 1),
        ('h_gate', 2, 1, 1, 0, 4, False),
        ('h_gate', 1, 1, 1, 0, 4, False),
        ('d_act', 0, 1, 2),
        ('d_act', 1, 1, 3),
        ('h_gate', 0, 1, 1, 0, 4, False),
        ('d_act', 0, 1, 3),
        ('d_mix', 1, 1),
        ('h_quant', 2, 1),
        ('h_quant', 1, 1),
        ('h_quant', 0, 1),
        ('y_grad', 0, 256, 256, 0),
        ('d_mix', 0, 1),
        ('y_grad', 0, 256, 256, 2),
        ('y_grad', 0, 0, 256, 0),
        ('d_act', 2, 1, 0),
        ('d_act', 2, 1, 1),
        ('d_quant', 1, 1),
        ('d_act', 2, 1, 3),
        ('y_sub', 0, 256, 256, 0, 4, False),
        ('d_quant', 0, 1),
        ('d_act', 2, 1, 2),
        ('y_grad', 1, 256, 256, 0),
        ('y_grad', 0, 0, 256, 2),
        ('y_grad', 1, 0, 256, 0),
        ('d_mix', 2, 1),
        ('y_grad', 1, 256, 256, 2),
        ('y_grad', 1, 0, 256, 2),
        ('y_sig', 0, 256, 256),
        ('y_sub', 1, 256, 256, 0, 4, False),
        ('d_quant', 2, 1),
        ('y_sub', 1, 0, 256, 0, 4, False),
        ('y_sub', 0, 0, 256, 0, 4, False),
        ('y_grad', 1, 512, 256, 0),
        ('y_sig', 0, 0, 256),
        ('y_mul', 0, 256, 256),
        ('y_grad', 0, 768, 256, 0),
        ('y_mul', 0, 0, 256),
        ('y_grad', 1, 896, 128, 0),
        ('y_sig', 1, 0, 256),
        ('y_grad', 0, 768, 256, 2),
        ('y_grad', 0, 512, 256, 0),
        ('y_mix', 0, 256, 256, False),
        ('y_grad', 1, 768, 128, 0),
        ('y_mix', 0, 0, 256, False),
        ('y_grad', 0, 512, 256, 2),
        ('y_sig', 1, 256, 256),
        ('y_sub', 1, 768, 128, 0, 4, False),
        ('y_quant', 0, 0, 256),
        ('y_quant', 0, 256, 256),
        ('y_mul', 1, 0, 256),
        ('y_sub', 0, 512, 256, 0, 4, False),
        ('y_sub', 0, 768, 256, 0, 4, False),
        ('y_sig', 1, 768, 128),
        ('y_mul', 1, 768, 128),
        ('y_sig', 0, 512, 256),
        ('y_sig', 0, 768, 256),
        ('y_grad', 1, 512, 256, 2),
        ('y_sub', 1, 896, 128, 0, 4, False),
        ('y_mul', 1, 256, 256),
        ('warm_up', ACT.Sigmoid),
        ('y_mix', 1, 0, 256, False),
        ('y_mul', 0, 512, 256),
        ('y_mix', 1, 768, 128, False),
        ('y_sub', 1, 512, 256, 0, 4, False),
        ('y_sig', 1, 896, 128),
        ('y_mul', 1, 896, 128),
        ('y_mix', 0, 512, 256, False),
        ('y_quant', 1, 0, 256),
        ('y_quant', 1, 768, 128),
        ('y_mul', 0, 768, 256),
        ('y_sig', 1, 512, 256),
        ('y_mix', 1, 896, 128, True),
        ('y_mix', 1, 256, 256, False),
        ('y_quant', 0, 512, 256),
        ('y_mix', 0, 768, 256, False),
        ('y_quant', 1, 896, 128),
        ('y_mul', 1, 512, 256),
        ('y_mix', 1, 512, 256, False),
        ('y_quant', 0, 768, 256),
        ('y_quant', 1, 256, 256),
        ('y_quant', 1, 512, 256),
        ('st_scales',)]


def tile_movement_pruning_masked_weight_k4_kernel(
    tc, x, a, token_gate, loss_weight, e_words, e_scales, b_words, b_scales, w, score, out_0, out_1, out_2
):
    nc = tc.nc
    with ExitStack() as ctx:
        keep = ctx.enter_context(tc.tile_pool(name="keep", bufs=1))
        work = ctx.enter_context(tc.tile_pool(name="work", bufs=2))
        ps_s = ctx.enter_context(tc.psum_pool(name="ps_s", bufs=4))
        ps_v = ctx.enter_context(tc.psum_pool(name="ps_v", bufs=4))
        ctx.enter_context(tc.manual_schedule())

        def kept(name, shape, dtype):
            return keep.tile(shape, dtype, name=name, align_bytes=64)

        def rot(name, shape, dtype, bufs):
            return work.tile(shape, dtype, name=name, tag=name, bufs=bufs, align_bytes=64)

        ident = kept("ident", [P, P], F32)
        perm = kept("perm", [P, P], F32)
        warm = kept("warm", [P, 2], F32)
        fac_rows = kept("fac_rows", [2 * NG, KP], BF16)
        fac_perm = kept("fac_perm", [P, 4, P], F32)
        fac = kept("fac", [P, 8, 4], F32)
        es_raw = kept("es_raw", [P, 2, TOK], U8)
        es = kept("es", [P, 2, TOK], U8)
        bs = kept("bs", [P, 2, DOUT], U8)
        e_raw = [kept("e_raw%d" % G, [P, 2, KP], U32) for G in range(NG)]
        eq = [kept("eq%d" % G, [P, 2, KP], U32) for G in range(NG)]
        bq = [kept("bq%d" % h, [P, 2, 2 * KP], U8) for h in range(2)]
        a_raw = [kept("a_raw%d" % g, [P, 4, KP], BF16) for g in range(2)]
        aq = [kept("aq%d" % g, [P, KP], U32) for g in range(2)]
        a_sc = [kept("a_sc%d" % g, [P, KP], U8) for g in range(2)]
        x_raw = [kept("x_raw%d" % G, [P, 4, FIN], BF16) for G in range(NG)]
        xq = [kept("xq%d" % G, [P, KP], U32) for G in range(NG)]
        x_sc = [kept("x_sc%d" % G, [P, KP], U8) for G in range(NG)]
        hq = {(G, g): kept("hq%d%d" % (G, g), [P, KP], U32) for G in range(NG) for g in range(2)}
        h_sc = {(G, g): kept("h_sc%d%d" % (G, g), [P, KP], U8) for G in range(NG) for g in range(2)}
        dq = {(G, h): kept("dq%d%d" % (G, h), [P, KP], U32) for G in range(NG) for h in range(2)}
        d_sc = {(G, h): kept("d_sc%d%d" % (G, h), [P, KP], U8) for G in range(NG) for h in range(2)}
        w_sb = [kept("w_sb%d" % g, [P, 4, DOUT], BF16) for g in range(2)]
        s_sb = [kept("s_sb%d" % g, [P, 4, DOUT], BF16) for g in range(2)]
        y_sc = kept("y_sc", [P, 2, DOUT], U8)
        live = {}

        def bank(pool, shape):
            return pool.tile(shape, F32, name="bank", tag="bank")

        def quantize(codes, scales, values):
            nc.vector.quantize_mx(out=codes.bitcast(FP8X4), scales=scales, in_=values.rearrange("p n t -> p (n t)"))

        def interleave(copy, dst, src):
            copy(out=dst.rearrange("p (c i) t -> p c t i", i=4), in_=src.rearrange("p t (c i) -> p c t i", i=4))

        def ld_fac():
            nc.scalar.dma_start(out=fac_rows[0:NG, :], in_=token_gate.rearrange("(g n) o -> g (n o)", g=NG))
            nc.scalar.dma_start(out=fac_rows[NG : 2 * NG, :], in_=loss_weight.rearrange("(g n) o -> g (n o)", g=NG))

        def ld_scales(plane, rows):
            for Q in range(4):
                nc.sync.dma_start(
                    out=plane[32 * Q : 32 * Q + 4, :, :].bitcast(I32),
                    in_=rows[:, 4 * Q : 4 * Q + 4, :].rearrange("g r n -> r g n").bitcast(I32),
                )

        def ld_es():
            ld_scales(es_raw, e_scales)

        def ld_bs():
            ld_scales(bs, b_scales)

        def ld_e(G):
            src = e_words.rearrange("g p n t -> p g (n t)")[:, :, 4 * KP * G : 4 * KP * (G + 1)]
            nc.sync.dma_start(out=e_raw[G][:].bitcast(I32), in_=src.bitcast(I32))

        def ld_b(h):
            src = b_words.rearrange("g p n -> p g n")[:, :, 2 * KP * h : 2 * KP * (h + 1)]
            nc.sync.dma_start(out=bq[h][:].bitcast(I32), in_=src.bitcast(I32))

        def ld_a(g):
            nc.sync.dma_start(out=a_raw[g][:], in_=a[:, KP * g : KP * (g + 1)].rearrange("(p j) n -> p j n", j=4))

        def ld_x(G):
            nc.sync.dma_start(out=x_raw[G][:], in_=x[KP * G : KP * (G + 1), :].rearrange("(j p) k -> p j k", j=4))

        def ld_ws(g):
            rows = slice(KP * g, KP * (g + 1))
            nc.sync.dma_start(out=w_sb[g][:], in_=w[rows, :].rearrange("(p t) n -> p t n", t=4))
            nc.sync.dma_start(out=s_sb[g][:], in_=score[rows, :].rearrange("(p t) n -> p t n", t=4))

        def setup():
            nc.vector.memset(es_raw[:].bitcast(I32), 0)
            nc.vector.memset(bs[:].bitcast(I32), 0)
            nc.vector.memset(fac_perm[:], 0.0)
            make_identity(nc, ident[:])
            nc.gpsimd.tensor_copy(
                out=perm[:].rearrange("p (t q r) -> p t q r", t=4, q=4),
                in_=ident[:].rearrange("p (q t r) -> p t q r", t=4, q=4),
            )

        def warm_up(func):
            nc.scalar.activation(out=warm[:, 1:2], in_=ident[:, 0:1], func=func)

        def fac_a():
            nc.vector.tensor_copy(
                out=fac_perm[0 : 2 * NG].rearrange("p t (q r) -> p t q r", r=8),
                in_=fac_rows[:].rearrange("p (q t r) -> p t q r", t=4, r=8),
            )
            ps = bank(ps_v, [P, 4, P])
            for t in range(4):
                nc.tensor.transpose(ps[:, t, :], fac_perm[:, t, :], perm[:])
            live["fac"] = ps

        def fac_b():
            nc.vector.tensor_copy(out=fac[:], in_=live["fac"][:, :, 0:8].rearrange("p t j -> p j t"))

        def es_perm():
            src = es_raw[:].rearrange("p g n -> p (g n)").bitcast(I32).rearrange("p (G q t r) -> p t G q r", q=16, t=4, r=2)
            dst = es[:].rearrange("p g n -> p (g n)").bitcast(I32).rearrange("p (G t q r) -> p t G q r", q=16, t=4, r=2)
            for t in range(4):
                nc.vector.tensor_copy(out=dst[:, t], in_=src[:, t])

        def e_perm(G):
            for g in range(2):
                nc.vector.tensor_copy(
                    out=eq[G][:, g, :].bitcast(I32).rearrange("p (t q r) -> p t q r", t=4, r=8),
                    in_=e_raw[G][:, g, :].bitcast(I32).rearrange("p (q t r) -> p t q r", t=4, r=8),
                )

        def x_turn(G, half):
            if half == 0:
                live["xg", G] = rot("mix", [P, KP, 4], BF16, MIX_BUFS)
            ps = bank(ps_s, [P, 2, 2, P])
            for jj in range(2):
                words = x_raw[G][:, 2 * half + jj, :].bitcast(F32)
                for u in range(2):
                    nc.tensor.transpose(ps[:, jj, u, :], words[:, u : 2 * P : 2], perm[:])
            dst = live["xg", G][:].rearrange("p n t -> p (n t)").bitcast(F32).rearrange("p (t j m u) -> p j t m u", t=4, j=4, u=2)
            for jj in range(2):
                nc.scalar.copy(out=dst[:, 2 * half + jj], in_=ps[:, jj].rearrange("p u (t m) -> p t m u", t=4))

        def x_quant(G):
            quantize(xq[G][:], x_sc[G][:], live["xg", G][:])

        def a_mix(g, on_vector):
            live["ag", g] = rot("mix", [P, KP, 4], BF16, MIX_BUFS)
            interleave(nc.vector.tensor_copy if on_vector else nc.scalar.copy, live["ag", g][:], a_raw[g][:])

        def a_quant(g):
            quantize(aq[g][:], a_sc[g][:], live["ag", g][:])

        def z_silu(G, g, c):
            if c % 2 == 0:
                live["silu", G, g, c // 2] = rot("wide", [P, 4, 64, 4], F32, WIDE_BUFS)
            ps = bank(ps_s, [P, 4, P])
            cols = slice(P * c, P * (c + 1))
            for t in range(4):
                tok = slice(P * t, P * (t + 1))
                nc.tensor.matmul_mx(
                    out=ps[:, t, :], lhsT=xq[G][:, tok].bitcast(FP8X4), lhsT_scale=x_sc[G][:, tok],
                    rhs=aq[g][:, cols].bitcast(FP8X4), rhs_scale=a_sc[g][:, cols], start=True, stop=True,
                )
            dst = live["silu", G, g, c // 2][:, :, 32 * (c % 2) : 32 * (c % 2 + 1), :]
            nc.scalar.activation(out=dst, in_=ps[:].rearrange("p t (m s) -> p s m t", s=4), func=ACT.Silu)

        def h_gate(G, g, half, s0, s1, on_pool):
            if ("hb", G, g) not in live:
                live["hb", G, g] = rot("mix", [P, KP, 4], BF16, MIX_BUFS)
            dst = live["hb", G, g][:].rearrange("p (s m) t -> p s m t", s=4)[:, s0:s1, 64 * half : 64 * (half + 1), :]
            eng = nc.gpsimd if on_pool else nc.vector
            eng.tensor_tensor(
                out=dst, in0=live["silu", G, g, half][:, s0:s1],
                in1=fac[:, G, :].unsqueeze(1).unsqueeze(1).to_broadcast([P, s1 - s0, 64, 4]), op=ALU.mult,
            )

        def h_quant(G, g):
            quantize(hq[G, g][:], h_sc[G, g][:], live["hb", G, g][:])

        def d_matmul(out, G, t, h, c0, n):
            tok = slice(P * t, P * (t + 1))
            for g in range(2):
                nc.tensor.matmul_mx(
                    out=out, lhsT=eq[G][:, g, tok].bitcast(FP8X4),
                    lhsT_scale=es[:, g, KP * G + P * t : KP * G + P * (t + 1)],
                    rhs=bq[h][:, g, 2 * c0 : 2 * (c0 + n)].bitcast(FP4X4),
                    rhs_scale=bs[:, g, KP * h + c0 : KP * h + c0 + n], start=(g == 0), stop=(g == 1),
                )

        def d_vec(G, h, c):
            if c == 0:
                live["db", G, h] = rot("mix", [P, KP, 4], BF16, MIX_BUFS)
            ps = bank(ps_v, [P, 4, P])
            for t in range(4):
                d_matmul(ps[:, t, :], G, t, h, P * c, P)
            nc.vector.tensor_tensor(
                out=live["db", G, h][:, P * c : P * (c + 1), :], in0=ps[:].rearrange("p t n -> p n t"),
                in1=fac[:, NG + G, :].unsqueeze(1).to_broadcast([P, P, 4]), op=ALU.mult,
            )

        def d_act(G, h, t):
            if t == 0:
                live["dt", G, h] = rot("dt", [P, 4, KP], BF16, 2)
            ps = bank(ps_s, [P, KP])
            d_matmul(ps[:], G, t, h, 0, KP)
            nc.scalar.activation(out=live["dt", G, h][:, t, :], in_=ps[:], func=ACT.Copy, scale=fac[:, NG + G, t : t + 1])

        def d_mix(G, h):
            live["db", G, h] = rot("mix", [P, KP, 4], BF16, MIX_BUFS)
            interleave(nc.scalar.copy, live["db", G, h][:], live["dt", G, h][:])

        def d_quant(G, h):
            quantize(dq[G, h][:], d_sc[G, h][:], live["db", G, h][:])

        def y_grad(g, c0, n, first):
            if first == 0:
                live["u", g, c0] = rot("wide", [P, 4, n], F32, WIDE_BUFS)
            u = live["u", g, c0]
            h, cols = c0 // KP, slice(c0 % KP, c0 % KP + n)
            per_bank = KP // n
            for s0 in (first,):
                ps = bank(ps_v, [P, per_bank, n])
                for s in range(s0, s0 + per_bank):
                    rows = slice(P * s, P * (s + 1))
                    for G in range(NG):
                        nc.tensor.matmul_mx(
                            out=ps[:, s - s0, :], lhsT=hq[G, g][:, rows].bitcast(FP8X4), lhsT_scale=h_sc[G, g][:, rows],
                            rhs=dq[G, h][:, cols].bitcast(FP8X4), rhs_scale=d_sc[G, h][:, cols],
                            start=(G == 0), stop=(G == NG - 1),
                        )
                nc.vector.tensor_tensor(
                    out=u[:, s0 : s0 + per_bank, :], in0=ps[:], in1=w_sb[g][:, s0 : s0 + per_bank, c0 : c0 + n], op=ALU.mult
                )

        def y_sub(g, c0, n, s0, s1, on_pool):
            v = live["u", g, c0][:, s0:s1, :]
            eng = nc.gpsimd if on_pool else nc.vector
            eng.tensor_tensor(out=v, in0=s_sb[g][:, s0:s1, c0 : c0 + n], in1=v, op=ALU.subtract)

        def y_sig(g, c0, n):
            m = live["u", g, c0]
            nc.scalar.activation(out=m[:], in_=m[:], func=ACT.Sigmoid)

        def y_mul(g, c0, n):
            y = live["u", g, c0]
            nc.vector.tensor_tensor(out=y[:], in0=y[:], in1=w_sb[g][:, :, c0 : c0 + n], op=ALU.mult)
            rows = out_0[KP * g : KP * (g + 1), c0 : c0 + n]
            nc.sync.dma_start(out=rows.rearrange("(p t) n -> p t n", t=4), in_=y[:])

        def y_mix(g, c0, n, on_vector):
            yb = rot("yb", [P, n, 4], BF16, 3)
            live["yb", g, c0] = yb
            interleave(nc.vector.tensor_copy if on_vector else nc.scalar.copy, yb[:], live["u", g, c0][:])

        def y_quant(g, c0, n):
            yq = rot("yq", [P, n], U32, 4)
            quantize(yq[:], y_sc[:, g, c0 : c0 + n], live["yb", g, c0][:])
            dst = out_1[g].rearrange("p n t -> p (n t)")[:, 4 * c0 : 4 * (c0 + n)]
            nc.sync.dma_start(out=dst.bitcast(I32), in_=yq[:].bitcast(I32))

        def st_scales():
            for Q in range(4):
                nc.sync.dma_start(
                    out=out_2[:, 4 * Q : 4 * Q + 4, :].rearrange("g r n -> r g n").bitcast(I32),
                    in_=y_sc[32 * Q : 32 * Q + 4, :, :].bitcast(I32),
                )

        steps = {
            "ld_fac": ld_fac, "ld_es": ld_es, "ld_bs": ld_bs, "ld_e": ld_e, "ld_b": ld_b, "ld_a": ld_a, "ld_x": ld_x,
            "ld_ws": ld_ws, "setup": setup, "warm_up": warm_up, "fac_a": fac_a, "fac_b": fac_b, "es_perm": es_perm,
            "e_perm": e_perm, "x_turn": x_turn, "x_quant": x_quant, "a_mix": a_mix, "a_quant": a_quant,
            "z_silu": z_silu, "h_gate": h_gate, "h_quant": h_quant, "d_vec": d_vec, "d_act": d_act, "d_mix": d_mix,
            "d_quant": d_quant, "y_grad": y_grad, "y_sub": y_sub, "y_sig": y_sig, "y_mul": y_mul, "y_mix": y_mix,
            "y_quant": y_quant, "st_scales": st_scales,
        }
        for step in order():
            steps[step[0]](*step[1:])
